import numpy as np
import ml_dtypes


def mxq(x, axis, fmt="e4m3"):
    dtype, down = {"e4m3": (ml_dtypes.float8_e4m3fn, 7), "e5m2": (ml_dtypes.float8_e5m2, 14)}[fmt]
    v = np.moveaxis(np.asarray(x, np.float32).astype(ml_dtypes.bfloat16).astype(np.float64), axis, -1)
    blocks = v.reshape(v.shape[:-1] + (-1, 32))
    amax = np.abs(blocks).max(-1, keepdims=True)
    byte = np.maximum(np.where(amax > 0, np.frexp(amax)[1] - 1 + 127, 0) - down, 1)
    scale = np.exp2(byte - 127.0)
    codes = (blocks / scale).astype(np.float32).astype(dtype).astype(np.float64)
    return np.moveaxis((codes * scale).reshape(v.shape), -1, axis)


WIDE = False


def mx_kscale(k):
    if not WIDE:
        return np.ones(k)
    levels = np.array([10, -10, 5, -5, 0])
    if k % 512:
        return np.exp2(np.random.permutation(np.resize(levels, k // 32))).repeat(32)
    a = np.empty((k // 512, 16))
    for p in range(k // 512):
        a[p, :8] = np.random.permutation(np.resize(levels, 8))
        for g in range(8):
            far = levels[np.abs(levels - a[p, g]) >= 10]
            a[p, g + 8] = far[np.random.randint(len(far))]
    return np.exp2(a.ravel()).repeat(32)


def f64(x):
    return np.asarray(x).astype(np.float64)


def striped8(idx):
    return np.asarray(idx).reshape(8, -1, 16).transpose(0, 2, 1).reshape(128, -1).astype(np.uint16)


def unstriped8(offs):
    return offs.reshape(8, 16, -1).transpose(0, 2, 1).reshape(8, -1).astype(np.int64)


def pick8(x, idx, run):
    r = np.arange(len(x))
    return x[r[:, None], idx[r % (8 * run) // run]]


E2M1 = np.array([0.0, 0.5, 1.0, 1.5, 2.0, 3.0, 4.0, 6.0, -0.0, -0.5, -1.0, -1.5, -2.0, -3.0, -4.0, -6.0])


def pack_weight(w, fmt):
    k, n = w.shape
    w = f64(np.asarray(w, np.float32).astype(ml_dtypes.bfloat16)).reshape(k // 32, 32, n)
    amax = np.abs(w).max(1)
    if fmt == "e4m3":
        byte = np.frexp(amax)[1] - 1 + 127 - 7
    else:
        mant, ex = np.frexp(amax / 6.0)
        byte = np.where(mant > 0.5, ex, ex - 1) + 127
    byte = np.clip(np.where(amax > 0, byte, 1), 1, 254)
    scaled = (w * np.exp2(127.0 - byte)[:, None, :]).reshape(k, n).astype(np.float32)
    by_word = np.ascontiguousarray(scaled.reshape(k // 512, 128, 4, n).transpose(0, 1, 3, 2))
    if fmt == "e4m3":
        words = by_word.astype(ml_dtypes.float8_e4m3fn).view(np.uint8)
    else:
        c = by_word.astype(ml_dtypes.float4_e2m1fn).view(np.uint8) & 0xF
        words = (c[..., 0::2] | (c[..., 1::2] << 4)).reshape(k // 512, 128, 2 * n)
    return np.ascontiguousarray(words), np.ascontiguousarray(byte.astype(np.uint8).reshape(k // 512, 16, n))


def unpack_weight(words, scales, fmt):
    g, _, n = scales.shape
    words = np.ascontiguousarray(words).reshape(g, 128, n, -1)
    if fmt == "e4m3":
        vals = words.view(ml_dtypes.float8_e4m3fn).astype(np.float64)
    else:
        nib = np.empty((g, 128, n, 4), np.uint8)
        nib[..., 0::2] = words & 0xF
        nib[..., 1::2] = words >> 4
        vals = E2M1[nib]
    vals = vals * np.repeat(np.exp2(scales.astype(np.float64) - 127.0), 8, axis=1)[..., None]
    return vals.transpose(0, 1, 3, 2).reshape(g * 512, n)


def sigmoid(v):
    return 1.0 / (1.0 + np.exp(-v))


D, K, T, U, X, I, J, Q = 512, 512, 1024, 1024, 1024, 512, 256, 128


def setup_inputs():
    n = np.random.standard_normal
    idx = np.stack([np.random.permutation(T)[:I] for _ in range(8)])
    idx2 = np.stack([np.random.permutation(U)[:I] for _ in range(8)])
    idx3 = np.stack([np.random.permutation(X)[:J] for _ in range(8)])
    idx4 = np.stack([np.random.permutation(X)[:I] for _ in range(8)])
    fd = mx_kscale(D)
    fk = mx_kscale(K)
    wqp = pack_weight(n((D, K)) * 1.0 / np.sqrt(D) * fd[:, None] * fk, "e4m3")
    keysp = pack_weight(n((K, T)) * 1.0 / np.sqrt(K) / fk[:, None], "e4m3")
    notesp = pack_weight(n((K, U)) * 1.0 / np.sqrt(K) / fk[:, None], "e2m1")
    usersp = pack_weight(n((D, X)) * 1.0 / np.sqrt(D) * fd[:, None], "e4m3")
    return {
        "states": (n((D, Q)) * 0.95 / fd[:, None]).astype(np.float32),
        "wq_words": wqp[0],
        "wq_scales": wqp[1],
        "keys_words": keysp[0],
        "keys_scales": keysp[1],
        "notes_words": notesp[0],
        "notes_scales": notesp[1],
        "users_words": usersp[0],
        "users_scales": usersp[1],
        "thr": (np.random.uniform(-0.6, 0.6, (Q, 1))).astype(np.float32),
        "slope": (np.random.uniform(1.0, 3.0, (Q, 1))).astype(np.float32),
        "offs": striped8(idx),
        "offs2": striped8(idx2),
        "offs3": striped8(idx3),
        "offs4": striped8(idx4),
    }


def reference(states, wq_words, wq_scales, keys_words, keys_scales, notes_words, notes_scales, users_words, users_scales, thr, slope, offs, offs2, offs3, offs4):
    idx = unstriped8(offs)
    idx2 = unstriped8(offs2)
    idx3 = unstriped8(offs3)
    idx4 = unstriped8(offs4)
    wqu = unpack_weight(wq_words, wq_scales, "e4m3")
    keysu = unpack_weight(keys_words, keys_scales, "e4m3")
    notesu = unpack_weight(notes_words, notes_scales, "e2m1")
    usersu = unpack_weight(users_words, users_scales, "e4m3")
    statesq = mxq(f64(states), 0, "e4m3")
    qv = wqu.T @ statesq
    qvq = mxq(qv, 0, "e4m3")
    a = qvq.T @ keysu
    b = qvq.T @ notesu
    c0 = statesq.T @ usersu
    s1 = sigmoid(pick8(a, idx, 16) * f64(slope) + f64(thr))
    w = pick8(b, idx2, 16) * s1
    p2 = w.reshape(Q, J, I // J).sum(axis=2)
    f1 = np.zeros((Q, X))
    f1[np.arange(Q)[:, None], idx3[np.arange(Q) % 128 // 16]] = p2
    cc = c0 + f1
    y = pick8(cc, idx4, 16)
    return y

@@ -1,0 +1,180 @@
+from contextlib import ExitStack
+
+import concourse.mybir as mybir
+
+D, K, T, U, X, I, J, Q = 512, 512, 1024, 1024, 1024, 512, 256, 128
+FLOPS = 2 * Q * (D * K + K * T + K * U + D * X)
+
+F32 = mybir.dt.float32
+BF16 = mybir.dt.bfloat16
+I32 = mybir.dt.int32
+U32 = mybir.dt.uint32
+U16 = mybir.dt.uint16
+U8 = mybir.dt.uint8
+FP8X4 = mybir.dt.float8_e4m3fn_x4
+FP4X4 = mybir.dt.float4_e2m1fn_x4
+ACT = mybir.ActivationFunctionType
+ALU = mybir.AluOpType
+
+P = 128
+PACK = 4
+BANK = 512
+CHUNK = 256
+POOL_COLS = 256
+LIST = 16
+
+
+def load_scale_rows(queue, scale_tile, scales, quadrants=range(4)):
+    for quadrant in quadrants:
+        queue.dma_start(
+            out=scale_tile[32 * quadrant : 32 * quadrant + 4, :].bitcast(I32),
+            in_=scales[0, 4 * quadrant : 4 * quadrant + 4, :].bitcast(I32),
+        )
+
+
+def fp8_words(words):
+    return words[0].rearrange("p n t -> p (n t)").bitcast(I32)
+
+
+def tile_attend_pairopen_madethree_kernel(
+    tc, states, wq_words, wq_scales, keys_words, keys_scales, notes_words, notes_scales,
+    users_words, users_scales, thr, slope, offs, offs2, offs3, offs4, out,
+):
+    nc = tc.nc
+    with ExitStack() as ctx:
+        sb = ctx.enter_context(tc.tile_pool(name="sb", bufs=1))
+        ps = ctx.enter_context(tc.psum_pool(name="ps", bufs=1))
+
+        token_list = sb.tile([P, I // LIST], U16, name="token_list")
+        note_list = sb.tile([P, I // LIST], U16, name="note_list")
+        pair_list = sb.tile([P, J // LIST], U16, name="pair_list")
+        user_list = sb.tile([P, I // LIST], U16, name="user_list")
+        slope_col = sb.tile([P, 1], F32, name="slope_col")
+        thr_col = sb.tile([P, 1], F32, name="thr_col")
+
+        states_raw = sb.tile([P, PACK, Q], F32, name="states_raw", align_bytes=64)
+        wq_raw = sb.tile([P, K], U32, name="wq_raw", align_bytes=64)
+        wq_raw_scale = sb.tile([P, K], U8, name="wq_raw_scale", align_bytes=64)
+        keys = sb.tile([P, T], U32, name="keys", align_bytes=64)
+        keys_scale = sb.tile([P, T], U8, name="keys_scale", align_bytes=64)
+        notes = sb.tile([P, 2 * U], U8, name="notes", align_bytes=64)
+        notes_scale = sb.tile([P, U], U8, name="notes_scale", align_bytes=64)
+        users = sb.tile([P, X], U32, name="users", align_bytes=64)
+        users_scale = sb.tile([P, X], U8, name="users_scale", align_bytes=64)
+        f1 = sb.tile([P, X], F32, name="f1", align_bytes=64)
+
+        for scale_tile in (wq_raw_scale, notes_scale, keys_scale, users_scale):
+            nc.vector.memset(scale_tile[:].bitcast(I32), 0)
+
+        nc.sync.dma_start(out=states_raw[:], in_=states.rearrange("(p j) q -> p j q", j=PACK))
+        load_scale_rows(nc.sync, wq_raw_scale, wq_scales, range(2))
+        load_scale_rows(nc.scalar, wq_raw_scale, wq_scales, range(2, 4))
+        nc.sync.dma_start(out=wq_raw[:].bitcast(I32), in_=fp8_words(wq_words))
+        load_scale_rows(nc.gpsimd, notes_scale, notes_scales, range(3))
+        nc.sync.dma_start(token_list[:], offs)
+        nc.sync.dma_start(out=slope_col[:], in_=slope)
+        nc.sync.dma_start(out=keys[:].bitcast(I32), in_=fp8_words(keys_words))
+        load_scale_rows(nc.sync, keys_scale, keys_scales)
+        nc.sync.dma_start(out=notes[:].bitcast(I32), in_=notes_words[0].bitcast(I32))
+        load_scale_rows(nc.sync, notes_scale, notes_scales, range(3, 4))
+        nc.sync.dma_start(out=thr_col[:], in_=thr)
+        nc.sync.dma_start(note_list[:], offs2)
+        nc.sync.dma_start(out=users[:].bitcast(I32), in_=fp8_words(users_words))
+        load_scale_rows(nc.sync, users_scale, users_scales)
+        nc.sync.dma_start(pair_list[:], offs3)
+        nc.sync.dma_start(user_list[:], offs4)
+
+        nc.vector.memset(f1[:], 0.0)
+        states_bf = sb.tile([P, Q, PACK], BF16, name="states_bf", align_bytes=64)
+        nc.vector.tensor_copy(
+            out=states_bf[:].rearrange("p (c i) t -> p c t i", i=4),
+            in_=states_raw[:].rearrange("p t (c i) -> p c t i", i=4),
+        )
+        wq_scale = sb.tile([P, PACK, P], U8, name="wq_scale", align_bytes=64)
+        nc.vector.tensor_copy(
+            out=wq_scale[:].rearrange("p t m -> p m t"),
+            in_=wq_raw_scale[:].rearrange("p (m t) -> p m t", t=PACK),
+        )
+        states_q = sb.tile([P, Q], U32, name="states_q", align_bytes=64)
+        states_scale = sb.tile([P, Q], U8, name="states_scale", align_bytes=64)
+        nc.vector.quantize_mx(
+            out=states_q[:].bitcast(FP8X4), scales=states_scale[:],
+            in_=states_bf[:].rearrange("p q t -> p (q t)"),
+        )
+        wq = sb.tile([P, PACK, P], U32, name="wq", align_bytes=64)
+        wq_by_m = wq[:].rearrange("p t m -> p m t")
+        wq_raw_by_m = wq_raw[:].rearrange("p (m t) -> p m t", t=PACK)
+        nc.scalar.copy(wq_by_m[:, :, :2], wq_raw_by_m[:, :, :2])
+        nc.vector.tensor_copy(out=wq_by_m[:, :, 2:], in_=wq_raw_by_m[:, :, 2:])
+
+        qv_ps = ps.tile([P, PACK, Q], F32, name="bank0")
+        for t in range(PACK):
+            nc.tensor.matmul_mx(
+                out=qv_ps[:, t, :], lhsT=wq[:, t, :].bitcast(FP8X4), lhsT_scale=wq_scale[:, t, :],
+                rhs=states_q[:].bitcast(FP8X4), rhs_scale=states_scale[:], start=True, stop=True,
+            )
+        qv_bf = sb.tile([P, Q, PACK], BF16, name="qv_bf", align_bytes=64)
+        nc.scalar.copy(qv_bf[:], qv_ps[:].rearrange("p t q -> p q t"))
+        qv_q = sb.tile([P, Q], U32, name="qv_q", align_bytes=64)
+        qv_scale = sb.tile([P, Q], U8, name="qv_scale", align_bytes=64)
+        nc.vector.quantize_mx(
+            out=qv_q[:].bitcast(FP8X4), scales=qv_scale[:],
+            in_=qv_bf[:].rearrange("p q t -> p (q t)"),
+        )
+
+        def scores(tags, width, rows_q, rows_scale, moving, moving_scale):
+            banks = []
+            for h, tag in enumerate(tags):
+                cols = slice(h * width, (h + 1) * width)
+                bank = ps.tile([P, width], F32, name=tag)
+                nc.tensor.matmul_mx(
+                    out=bank[:], lhsT=rows_q[:].bitcast(FP8X4), lhsT_scale=rows_scale[:],
+                    rhs=moving(cols), rhs_scale=moving_scale[:, cols], start=True, stop=True,
+                )
+                banks.append((cols, bank))
+            return banks
+
+        a = sb.tile([P, T], F32, name="a", align_bytes=64)
+        b = sb.tile([P, U], F32, name="b", align_bytes=64)
+        a_ps = scores(["bank1", "bank2", "bank3", "bank4"], CHUNK, qv_q, qv_scale,
+                      lambda cols: keys[:, cols].bitcast(FP8X4), keys_scale)
+        b_ps = scores(["bank5", "bank6", "bank7", "bank0"], CHUNK, qv_q, qv_scale,
+                      lambda cols: notes[:, 2 * cols.start : 2 * cols.stop].bitcast(FP4X4), notes_scale)
+        for cols, bank in a_ps:
+            nc.scalar.copy(a[:, cols], bank[:])
+        for cols, bank in b_ps:
+            nc.vector.tensor_copy(out=b[:, cols], in_=bank[:])
+        c_ps = scores(["bank1", "bank2"], BANK, states_q, states_scale,
+                      lambda cols: users[:, cols].bitcast(FP8X4), users_scale)
+
+        half_i = I // 2
+        half_list = half_i // LIST
+        s1 = sb.tile([P, I], F32, name="s1", align_bytes=64)
+        nc.scalar.activation(s1[:], a[:].indirect(token_list[:]), ACT.Sigmoid, bias=thr_col[:], scale=slope_col[:])
+        b_listed = sb.tile([P, I], F32, name="b_listed", align_bytes=64)
+        nc.vector.tensor_copy(b_listed[:, :half_i], b[:].indirect(note_list[:, :half_list]))
+        nc.scalar.activation(b_listed[:, half_i:], b[:].indirect(note_list[:, half_list:]), ACT.Copy)
+
+        w = sb.tile([P, 2, J], F32, name="w", align_bytes=64)
+        nc.vector.tensor_tensor(
+            w[:].rearrange("p e j -> p j e"),
+            b_listed[:].rearrange("p (j e) -> p j e", e=2),
+            s1[:].rearrange("p (j e) -> p j e", e=2),
+            ALU.mult,
+        )
+        nc.vector.tensor_tensor(f1[:].indirect(pair_list[:]), w[:, 0, :], w[:, 1, :], ALU.add)
+
+        cc = sb.tile([P, X], F32, name="cc", align_bytes=64)
+        split = X - POOL_COLS
+        c_tail = sb.tile([P, POOL_COLS], F32, name="c_tail", align_bytes=64)
+        nc.scalar.copy(c_tail[:], c_ps[1][1][:, BANK - POOL_COLS :])
+        nc.gpsimd.tensor_tensor(cc[:, split:], c_tail[:], f1[:, split:], ALU.add)
+        nc.vector.tensor_tensor(cc[:, :BANK], c_ps[0][1][:], f1[:, :BANK], ALU.add)
+        nc.vector.tensor_tensor(cc[:, BANK:split], c_ps[1][1][:, : BANK - POOL_COLS], f1[:, BANK:split], ALU.add)
+
+        y0 = sb.tile([P, half_i], F32, name="y0", align_bytes=64)
+        y1 = sb.tile([P, half_i], F32, name="y1", align_bytes=64)
+        nc.vector.tensor_copy(y0[:], cc[:].indirect(user_list[:, :half_list]))
+        nc.scalar.activation(y1[:], cc[:].indirect(user_list[:, half_list:]), ACT.Copy)
+        nc.sync.dma_start(out=out[:, :half_i], in_=y0[:])
+        nc.scalar.dma_start(out=out[:, half_i:], in_=y1[:])

@@ -84,6 +84,11 @@ def tile_attend_pairopen_madethree_kernel(
         nc.sync.dma_start(pair_list[:], offs3)
         nc.sync.dma_start(user_list[:], offs4)
 
+        warm_in = sb.tile([P, 1], F32, name="warm_in")
+        warm_out = sb.tile([P, 1], F32, name="warm_out")
+        nc.vector.memset(warm_in[:], 0.0)
+        nc.scalar.activation(warm_out[:], warm_in[:], ACT.Sigmoid)
+
         nc.vector.memset(f1[:], 0.0)
         states_bf = sb.tile([P, Q, PACK], BF16, name="states_bf", align_bytes=64)
         nc.vector.tensor_copy(

@@ -19,7 +19,6 @@ ALU = mybir.AluOpType
 P = 128
 PACK = 4
 BANK = 512
-CHUNK = 256
 POOL_COLS = 256
 LIST = 16
 
@@ -70,13 +69,13 @@ def tile_attend_pairopen_madethree_kernel(
         load_scale_rows(nc.sync, wq_raw_scale, wq_scales, range(2))
         load_scale_rows(nc.scalar, wq_raw_scale, wq_scales, range(2, 4))
         nc.sync.dma_start(out=wq_raw[:].bitcast(I32), in_=fp8_words(wq_words))
-        load_scale_rows(nc.gpsimd, notes_scale, notes_scales, range(3))
-        nc.sync.dma_start(token_list[:], offs)
-        nc.sync.dma_start(out=slope_col[:], in_=slope)
+        load_scale_rows(nc.gpsimd, notes_scale, notes_scales, range(2))
         nc.sync.dma_start(out=keys[:].bitcast(I32), in_=fp8_words(keys_words))
         load_scale_rows(nc.sync, keys_scale, keys_scales)
         nc.sync.dma_start(out=notes[:].bitcast(I32), in_=notes_words[0].bitcast(I32))
-        load_scale_rows(nc.sync, notes_scale, notes_scales, range(3, 4))
+        load_scale_rows(nc.sync, notes_scale, notes_scales, range(2, 4))
+        nc.sync.dma_start(token_list[:], offs)
+        nc.sync.dma_start(out=slope_col[:], in_=slope)
         nc.sync.dma_start(out=thr_col[:], in_=thr)
         nc.sync.dma_start(note_list[:], offs2)
         nc.sync.dma_start(out=users[:].bitcast(I32), in_=fp8_words(users_words))
@@ -97,8 +96,8 @@ def tile_attend_pairopen_madethree_kernel(
         )
         wq_scale = sb.tile([P, PACK, P], U8, name="wq_scale", align_bytes=64)
         nc.vector.tensor_copy(
-            out=wq_scale[:].rearrange("p t m -> p m t"),
-            in_=wq_raw_scale[:].rearrange("p (m t) -> p m t", t=PACK),
+            out=wq_scale[:],
+            in_=wq_raw_scale[:].rearrange("p (m t) -> p t m", t=PACK),
         )
         states_q = sb.tile([P, Q], U32, name="states_q", align_bytes=64)
         states_scale = sb.tile([P, Q], U8, name="states_scale", align_bytes=64)
@@ -127,10 +126,12 @@ def tile_attend_pairopen_madethree_kernel(
             in_=qv_bf[:].rearrange("p q t -> p (q t)"),
         )
 
-        def scores(tags, width, rows_q, rows_scale, moving, moving_scale):
+        def scores(tags, widths, rows_q, rows_scale, moving, moving_scale):
             banks = []
-            for h, tag in enumerate(tags):
-                cols = slice(h * width, (h + 1) * width)
+            start = 0
+            for tag, width in zip(tags, widths):
+                cols = slice(start, start + width)
+                start = start + width
                 bank = ps.tile([P, width], F32, name=tag)
                 nc.tensor.matmul_mx(
                     out=bank[:], lhsT=rows_q[:].bitcast(FP8X4), lhsT_scale=rows_scale[:],
@@ -141,15 +142,15 @@ def tile_attend_pairopen_madethree_kernel(
 
         a = sb.tile([P, T], F32, name="a", align_bytes=64)
         b = sb.tile([P, U], F32, name="b", align_bytes=64)
-        a_ps = scores(["bank1", "bank2", "bank3", "bank4"], CHUNK, qv_q, qv_scale,
+        a_ps = scores(["bank1", "bank2", "bank3", "bank4"], [256] * 4, qv_q, qv_scale,
                       lambda cols: keys[:, cols].bitcast(FP8X4), keys_scale)
-        b_ps = scores(["bank5", "bank6", "bank7", "bank0"], CHUNK, qv_q, qv_scale,
-                      lambda cols: notes[:, 2 * cols.start : 2 * cols.stop].bitcast(FP4X4), notes_scale)
         for cols, bank in a_ps:
             nc.scalar.copy(a[:, cols], bank[:])
+        b_ps = scores(["bank5", "bank6", "bank7", "bank0", "bank1"], [256, 256, 256, 128, 128], qv_q, qv_scale,
+                      lambda cols: notes[:, 2 * cols.start : 2 * cols.stop].bitcast(FP4X4), notes_scale)
         for cols, bank in b_ps:
             nc.vector.tensor_copy(out=b[:, cols], in_=bank[:])
-        c_ps = scores(["bank1", "bank2"], BANK, states_q, states_scale,
+        c_ps = scores(["bank7", "bank0"], [BANK] * 2, states_q, states_scale,
                       lambda cols: users[:, cols].bitcast(FP8X4), users_scale)
 
         half_i = I // 2
@@ -162,9 +163,9 @@ def tile_attend_pairopen_madethree_kernel(
 
         w = sb.tile([P, 2, J], F32, name="w", align_bytes=64)
         nc.vector.tensor_tensor(
-            w[:].rearrange("p e j -> p j e"),
-            b_listed[:].rearrange("p (j e) -> p j e", e=2),
-            s1[:].rearrange("p (j e) -> p j e", e=2),
+            w[:].rearrange("p e (c i) -> p c e i", i=4),
+            b_listed[:].rearrange("p (c i e) -> p c e i", i=4, e=2),
+            s1[:].rearrange("p (c i e) -> p c e i", i=4, e=2),
             ALU.mult,
         )
         nc.vector.tensor_tensor(f1[:].indirect(pair_list[:]), w[:, 0, :], w[:, 1, :], ALU.add)

from contextlib import ExitStack

import concourse.mybir as mybir

D, K, T, U, X, I, J, Q = 512, 512, 1024, 1024, 1024, 512, 256, 128
FLOPS = 2 * Q * (D * K + K * T + K * U + D * X)

F32 = mybir.dt.float32
BF16 = mybir.dt.bfloat16
I32 = mybir.dt.int32
U32 = mybir.dt.uint32
U16 = mybir.dt.uint16
U8 = mybir.dt.uint8
FP8X4 = mybir.dt.float8_e4m3fn_x4
FP4X4 = mybir.dt.float4_e2m1fn_x4
ACT = mybir.ActivationFunctionType
ALU = mybir.AluOpType

P = 128
PACK = 4
BANK = 512
POOL_COLS = 256
LIST = 16


def load_scale_rows(queue, scale_tile, scales, quadrants=range(4)):
    for quadrant in quadrants:
        queue.dma_start(
            out=scale_tile[32 * quadrant : 32 * quadrant + 4, :].bitcast(I32),
            in_=scales[0, 4 * quadrant : 4 * quadrant + 4, :].bitcast(I32),
        )


def fp8_words(words):
    return words[0].rearrange("p n t -> p (n t)").bitcast(I32)


def tile_attend_pairopen_madethree_kernel(
    tc, states, wq_words, wq_scales, keys_words, keys_scales, notes_words, notes_scales,
    users_words, users_scales, thr, slope, offs, offs2, offs3, offs4, out,
):
    nc = tc.nc
    with ExitStack() as ctx:
        sb = ctx.enter_context(tc.tile_pool(name="sb", bufs=1))
        ps = ctx.enter_context(tc.psum_pool(name="ps", bufs=1))

        token_list = sb.tile([P, I // LIST], U16, name="token_list")
        note_list = sb.tile([P, I // LIST], U16, name="note_list")
        pair_list = sb.tile([P, J // LIST], U16, name="pair_list")
        user_list = sb.tile([P, I // LIST], U16, name="user_list")
        slope_col = sb.tile([P, 1], F32, name="slope_col")
        thr_col = sb.tile([P, 1], F32, name="thr_col")

        states_raw = sb.tile([P, PACK, Q], F32, name="states_raw", align_bytes=64)
        wq_raw = sb.tile([P, K], U32, name="wq_raw", align_bytes=64)
        wq_raw_scale = sb.tile([P, K], U8, name="wq_raw_scale", align_bytes=64)
        keys = sb.tile([P, T], U32, name="keys", align_bytes=64)
        keys_scale = sb.tile([P, T], U8, name="keys_scale", align_bytes=64)
        notes = sb.tile([P, 2 * U], U8, name="notes", align_bytes=64)
        notes_scale = sb.tile([P, U], U8, name="notes_scale", align_bytes=64)
        users = sb.tile([P, X], U32, name="users", align_bytes=64)
        users_scale = sb.tile([P, X], U8, name="users_scale", align_bytes=64)
        f1 = sb.tile([P, X], F32, name="f1", align_bytes=64)

        for scale_tile in (wq_raw_scale, notes_scale, keys_scale, users_scale):
            nc.vector.memset(scale_tile[:].bitcast(I32), 0)

        nc.sync.dma_start(out=states_raw[:], in_=states.rearrange("(p j) q -> p j q", j=PACK))
        load_scale_rows(nc.sync, wq_raw_scale, wq_scales, range(2))
        load_scale_rows(nc.scalar, wq_raw_scale, wq_scales, range(2, 4))
        nc.sync.dma_start(out=wq_raw[:].bitcast(I32), in_=fp8_words(wq_words))
        load_scale_rows(nc.gpsimd, notes_scale, notes_scales, range(2))
        nc.sync.dma_start(out=keys[:].bitcast(I32), in_=fp8_words(keys_words))
        load_scale_rows(nc.sync, keys_scale, keys_scales)
        nc.sync.dma_start(out=notes[:].bitcast(I32), in_=notes_words[0].bitcast(I32))
        load_scale_rows(nc.sync, notes_scale, notes_scales, range(2, 4))
        nc.sync.dma_start(token_list[:], offs)
        nc.sync.dma_start(out=slope_col[:], in_=slope)
        nc.sync.dma_start(out=thr_col[:], in_=thr)
        nc.sync.dma_start(note_list[:], offs2)
        nc.sync.dma_start(out=users[:].bitcast(I32), in_=fp8_words(users_words))
        load_scale_rows(nc.sync, users_scale, users_scales)
        nc.sync.dma_start(pair_list[:], offs3)
        nc.sync.dma_start(user_list[:], offs4)

        warm_in = sb.tile([P, 1], F32, name="warm_in")
        warm_out = sb.tile([P, 1], F32, name="warm_out")
        nc.vector.memset(warm_in[:], 0.0)
        nc.scalar.activation(warm_out[:], warm_in[:], ACT.Sigmoid)

        nc.vector.memset(f1[:], 0.0)
        states_bf = sb.tile([P, Q, PACK], BF16, name="states_bf", align_bytes=64)
        nc.vector.tensor_copy(
            out=states_bf[:].rearrange("p (c i) t -> p c t i", i=4),
            in_=states_raw[:].rearrange("p t (c i) -> p c t i", i=4),
        )
        wq_scale = sb.tile([P, PACK, P], U8, name="wq_scale", align_bytes=64)
        nc.vector.tensor_copy(
            out=wq_scale[:],
            in_=wq_raw_scale[:].rearrange("p (m t) -> p t m", t=PACK),
        )
        states_q = sb.tile([P, Q], U32, name="states_q", align_bytes=64)
        states_scale = sb.tile([P, Q], U8, name="states_scale", align_bytes=64)
        nc.vector.quantize_mx(
            out=states_q[:].bitcast(FP8X4), scales=states_scale[:],
            in_=states_bf[:].rearrange("p q t -> p (q t)"),
        )
        wq = sb.tile([P, PACK, P], U32, name="wq", align_bytes=64)
        wq_by_m = wq[:].rearrange("p t m -> p m t")
        wq_raw_by_m = wq_raw[:].rearrange("p (m t) -> p m t", t=PACK)
        nc.scalar.copy(wq_by_m[:, :, :2], wq_raw_by_m[:, :, :2])
        nc.vector.tensor_copy(out=wq_by_m[:, :, 2:], in_=wq_raw_by_m[:, :, 2:])

        qv_ps = ps.tile([P, PACK, Q], F32, name="bank0")
        for t in range(PACK):
            nc.tensor.matmul_mx(
                out=qv_ps[:, t, :], lhsT=wq[:, t, :].bitcast(FP8X4), lhsT_scale=wq_scale[:, t, :],
                rhs=states_q[:].bitcast(FP8X4), rhs_scale=states_scale[:], start=True, stop=True,
            )
        qv_bf = sb.tile([P, Q, PACK], BF16, name="qv_bf", align_bytes=64)
        nc.scalar.copy(qv_bf[:], qv_ps[:].rearrange("p t q -> p q t"))
        qv_q = sb.tile([P, Q], U32, name="qv_q", align_bytes=64)
        qv_scale = sb.tile([P, Q], U8, name="qv_scale", align_bytes=64)
        nc.vector.quantize_mx(
            out=qv_q[:].bitcast(FP8X4), scales=qv_scale[:],
            in_=qv_bf[:].rearrange("p q t -> p (q t)"),
        )

        def scores(tags, widths, rows_q, rows_scale, moving, moving_scale):
            banks = []
            start = 0
            for tag, width in zip(tags, widths):
                cols = slice(start, start + width)
                start = start + width
                bank = ps.tile([P, width], F32, name=tag)
                nc.tensor.matmul_mx(
                    out=bank[:], lhsT=rows_q[:].bitcast(FP8X4), lhsT_scale=rows_scale[:],
                    rhs=moving(cols), rhs_scale=moving_scale[:, cols], start=True, stop=True,
                )
                banks.append((cols, bank))
            return banks

        a = sb.tile([P, T], F32, name="a", align_bytes=64)
        b = sb.tile([P, U], F32, name="b", align_bytes=64)
        a_ps = scores(["bank1", "bank2", "bank3", "bank4"], [256] * 4, qv_q, qv_scale,
                      lambda cols: keys[:, cols].bitcast(FP8X4), keys_scale)
        for cols, bank in a_ps:
            nc.scalar.copy(a[:, cols], bank[:])
        b_ps = scores(["bank5", "bank6", "bank7", "bank0", "bank1"], [256, 256, 256, 128, 128], qv_q, qv_scale,
                      lambda cols: notes[:, 2 * cols.start : 2 * cols.stop].bitcast(FP4X4), notes_scale)
        for cols, bank in b_ps:
            nc.vector.tensor_copy(out=b[:, cols], in_=bank[:])
        c_ps = scores(["bank7", "bank0"], [BANK] * 2, states_q, states_scale,
                      lambda cols: users[:, cols].bitcast(FP8X4), users_scale)

        half_i = I // 2
        half_list = half_i // LIST
        s1 = sb.tile([P, I], F32, name="s1", align_bytes=64)
        nc.scalar.activation(s1[:], a[:].indirect(token_list[:]), ACT.Sigmoid, bias=thr_col[:], scale=slope_col[:])
        b_listed = sb.tile([P, I], F32, name="b_listed", align_bytes=64)
        nc.vector.tensor_copy(b_listed[:, :half_i], b[:].indirect(note_list[:, :half_list]))
        nc.scalar.activation(b_listed[:, half_i:], b[:].indirect(note_list[:, half_list:]), ACT.Copy)

        w = sb.tile([P, 2, J], F32, name="w", align_bytes=64)
        nc.vector.tensor_tensor(
            w[:].rearrange("p e (c i) -> p c e i", i=4),
            b_listed[:].rearrange("p (c i e) -> p c e i", i=4, e=2),
            s1[:].rearrange("p (c i e) -> p c e i", i=4, e=2),
            ALU.mult,
        )
        nc.vector.tensor_tensor(f1[:].indirect(pair_list[:]), w[:, 0, :], w[:, 1, :], ALU.add)

        cc = sb.tile([P, X], F32, name="cc", align_bytes=64)
        split = X - POOL_COLS
        c_tail = sb.tile([P, POOL_COLS], F32, name="c_tail", align_bytes=64)
        nc.scalar.copy(c_tail[:], c_ps[1][1][:, BANK - POOL_COLS :])
        nc.gpsimd.tensor_tensor(cc[:, split:], c_tail[:], f1[:, split:], ALU.add)
        nc.vector.tensor_tensor(cc[:, :BANK], c_ps[0][1][:], f1[:, :BANK], ALU.add)
        nc.vector.tensor_tensor(cc[:, BANK:split], c_ps[1][1][:, : BANK - POOL_COLS], f1[:, BANK:split], ALU.add)

        y0 = sb.tile([P, half_i], F32, name="y0", align_bytes=64)
        y1 = sb.tile([P, half_i], F32, name="y1", align_bytes=64)
        nc.vector.tensor_copy(y0[:], cc[:].indirect(user_list[:, :half_list]))
        nc.scalar.activation(y1[:], cc[:].indirect(user_list[:, half_list:]), ACT.Copy)
        nc.sync.dma_start(out=out[:, :half_i], in_=y0[:])
        nc.scalar.dma_start(out=out[:, half_i:], in_=y1[:])
